import numpy as np, ml_dtypes
CORES = [51,54,179,182]
N = 4
DEG, TK = 3, 512
MASK = [[0,3,1],[0,3,1],[0,3,2],[0,3,1]]
def setup_inputs(rng):
    return {"x": rng.standard_normal((N, 128, TK), dtype=np.float32).astype(ml_dtypes.bfloat16), "w": rng.standard_normal((N, 128, DEG * 128), dtype=np.float32).astype(ml_dtypes.bfloat16)}
def setup_inputs_big(rng):
    d = setup_inputs(rng)
    for k in ("x", "w"): d[k] = (d[k].astype(np.float32) * 1024.0).astype(d[k].dtype)
    return d
def setup_inputs_small(rng):
    d = setup_inputs(rng)
    for k in ("x", "w"): d[k] = (d[k].astype(np.float32) * (1 / 1024.0)).astype(d[k].dtype)
    return d
def setup_inputs_apart(rng):
    d = setup_inputs(rng)
    f = (10.0 ** rng.permutation(np.linspace(-1.5, 1.5, N))).astype(np.float32).reshape(N, 1, 1)
    for k in ("x", "w"): d[k] = (d[k].astype(np.float32) * f).astype(d[k].dtype)
    return d
def reference(x, w):
    X, W = x.astype(np.float64), w.astype(np.float64)
    y = np.zeros((N, 128, TK))
    for r in range(N):
        for i, j in enumerate(MASK[r]):
            y[r] += W[r][:, 128 * i:128 * i + 128].T @ X[j]
    return {"y": y.astype(ml_dtypes.bfloat16 if x.dtype != np.float64 else np.float64)}

@@ -1,0 +1,117 @@
+from concourse.bass import DstId, RemoteDMATransfer
+
+DEG, TILE, TK = 3, 128, 512
+PIECES = 2
+CW = TK // PIECES
+
+SCRATCH = {
+    "xs": ("sbuf", [128, TK], "bfloat16"),
+    "ws": ("sbuf", [128, DEG * TILE], "bfloat16"),
+    "ys": ("sbuf", [128, TK], "bfloat16"),
+}
+for _i in range(DEG):
+    SCRATCH["in%d" % _i] = ("sbuf", [128, TK], "bfloat16")
+for _p in range(PIECES):
+    SCRATCH["ps%d" % _p] = ("psum", [128, 512], "float32")
+
+SEMAPHORES = (["ldx", "ldw", "sent", "cp", "st"] + ["arr%d" % _i for _i in range(DEG)]
+              + ["mm%d" % _p for _p in range(PIECES)])
+
+
+def _bits(m):
+    return [b for b in range(m.bit_length()) if (m >> b) & 1]
+
+
+def _pow2(n):
+    p = 1
+    while 2 * p <= n:
+        p *= 2
+    return p
+
+
+def _same_chip(topo, a, b):
+    return (topo.host(a), topo.chip(a)) == (topo.host(b), topo.chip(b))
+
+
+def _plan(T, topo, j):
+    mask, cores = T.tables["MASK"], T.cores
+    src = cores[j]
+    dests = [r for r in range(len(cores)) if r != j and j in mask[r]]
+    far = [r for r in dests if not _same_chip(topo, src, cores[r])]
+    near = [r for r in dests if _same_chip(topo, src, cores[r])]
+    used, calls = [], []
+    for group in (far, near):
+        if not group:
+            continue
+        free = [e for e in _bits(topo.mask(src, cores[group[0]])) if e not in used]
+        for r in group[1:]:
+            free = [e for e in free if e in _bits(topo.mask(src, cores[r]))]
+        n = _pow2(len(free) // len(group))
+        call = []
+        for k, r in enumerate(group):
+            eng = free[k * n:(k + 1) * n]
+            used += eng
+            call.append((r, mask[r].index(j), eng))
+        calls.append(call)
+    return calls
+
+
+def rank_program(g, core, T, topo):
+    r = T.rank_of(core)
+    if r is None:
+        return
+    mask, cores, sem = T.tables["MASK"], T.cores, T.sem
+    calls = _plan(T, topo, r)
+
+    if calls or r in mask[r]:
+        g.sync.dma_start(T.xs[:], T.x[:]).then_inc(sem.ldx, 16)
+    g.sync.dma_start(T.ws[:], T.w[:]).then_inc(sem.ldw, 16)
+
+    if calls:
+        g.wait_ge(sem.ldx, 16)
+        total = 0
+        for call in calls:
+            trs = []
+            for d, slot, eng in call:
+                rid, pid = topo.addr(cores[d], core)
+                trs.append(RemoteDMATransfer(dst_ids=[DstId(rid=rid, pnc=pid)],
+                                             dma_engine_mask=sum(1 << e for e in eng),
+                                             remote_sem=sem["arr%d" % slot],
+                                             src=T.xs[:], dst=T["in%d" % slot][:]))
+                total += len(eng)
+            g.remote_dma_fused(trs, local_sem=sem.sent)
+        g.wait_ge(sem.sent, total)
+
+    terms = []
+    for i, j in enumerate(mask[r]):
+        if j == r:
+            terms.append((0, 0, i, 0))
+            continue
+        for call in _plan(T, topo, j):
+            for d, slot, eng in call:
+                if d == r:
+                    terms.append((1 if _same_chip(topo, cores[j], core) else 2, 128 // len(eng), i, len(eng)))
+    terms.sort()
+
+    te = g.tensor
+    te.wait_ge(sem.ldw, 16)
+    for k, (_, _, i, cnt) in enumerate(terms):
+        if cnt == 0:
+            te.wait_ge(sem.ldx, 16)
+            rhs = T.xs
+        else:
+            te.wait_ge(sem["arr%d" % i], cnt)
+            rhs = T["in%d" % i]
+        last = k == len(terms) - 1
+        for p in range(PIECES):
+            ins = te.matmul(T["ps%d" % p][:, 0:CW], T.ws[:, TILE * i:TILE * (i + 1)], rhs[:, p * CW:(p + 1) * CW],
+                            k == 0, last)
+            if last:
+                ins.then_inc(sem["mm%d" % p], 1)
+
+    for p in range(PIECES):
+        g.vector.wait_ge(sem["mm%d" % p], 1)
+        g.vector.tensor_copy(T.ys[:, p * CW:(p + 1) * CW], T["ps%d" % p][:, 0:CW]).then_inc(sem.cp, 1)
+    g.sync.wait_ge(sem.cp, PIECES)
+    g.sync.dma_start(T.y[:], T.ys[:]).then_inc(sem.st, 16)
+    g.sync.wait_ge(sem.st, 16)

@@ -1,8 +1,9 @@
 from concourse.bass import DstId, RemoteDMATransfer
 
 DEG, TILE, TK = 3, 128, 512
-PIECES = 2
-CW = TK // PIECES
+HALF = TK // 2
+PW = 128
+NP = TK // PW
 
 SCRATCH = {
     "xs": ("sbuf", [128, TK], "bfloat16"),
@@ -11,11 +12,12 @@ SCRATCH = {
 }
 for _i in range(DEG):
     SCRATCH["in%d" % _i] = ("sbuf", [128, TK], "bfloat16")
-for _p in range(PIECES):
+for _p in range(NP):
     SCRATCH["ps%d" % _p] = ("psum", [128, 512], "float32")
 
-SEMAPHORES = (["ldx", "ldw", "sent", "cp", "st"] + ["arr%d" % _i for _i in range(DEG)]
-              + ["mm%d" % _p for _p in range(PIECES)])
+SEMAPHORES = (["ldx0", "ldx1", "ldw", "sent", "cp0", "cp1", "st"]
+              + ["a%d%d" % (_i, _c) for _i in range(DEG) for _c in range(2)]
+              + ["mm%d" % _p for _p in range(NP)])
 
 
 def _bits(m):
@@ -29,31 +31,70 @@ def _pow2(n):
     return p
 
 
-def _same_chip(topo, a, b):
-    return (topo.host(a), topo.chip(a)) == (topo.host(b), topo.chip(b))
+def _share(engines, k):
+    n = _pow2(len(engines) // k)
+    return [engines[i * n:(i + 1) * n] for i in range(k)]
 
 
-def _plan(T, topo, j):
+def _plan(T, topo):
     mask, cores = T.tables["MASK"], T.cores
-    src = cores[j]
-    dests = [r for r in range(len(cores)) if r != j and j in mask[r]]
-    far = [r for r in dests if not _same_chip(topo, src, cores[r])]
-    near = [r for r in dests if _same_chip(topo, src, cores[r])]
-    used, calls = [], []
-    for group in (far, near):
-        if not group:
-            continue
-        free = [e for e in _bits(topo.mask(src, cores[group[0]])) if e not in used]
-        for r in group[1:]:
-            free = [e for e in free if e in _bits(topo.mask(src, cores[r]))]
-        n = _pow2(len(free) // len(group))
-        call = []
-        for k, r in enumerate(group):
-            eng = free[k * n:(k + 1) * n]
-            used += eng
-            call.append((r, mask[r].index(j), eng))
-        calls.append(call)
-    return calls
+    n = len(cores)
+
+    def place(c):
+        return (topo.host(c), topo.chip(c))
+
+    users = [[r for r in range(n) if r != j and j in mask[r]] for j in range(n)]
+    calls, later, lands, offchip = [[] for _ in range(n)], [[] for _ in range(n)], [[] for _ in range(n)], []
+    for j in range(n):
+        eng = None
+        for r in users[j]:
+            if place(cores[r]) != place(cores[j]):
+                b = _bits(topo.mask(cores[j], cores[r]))
+                eng = b if eng is None else [e for e in eng if e in b]
+        offchip.append(eng or [])
+
+    def onchip(q, dsts):
+        eng = _bits(topo.mask(cores[q], cores[dsts[0]]))
+        for d in dsts[1:]:
+            eng = [e for e in eng if e in _bits(topo.mask(cores[q], cores[d]))]
+        return [e for e in eng if e not in offchip[q]] or eng
+
+    def move(q, buf, j, r, c0, c1, eng, key):
+        slot = mask[r].index(j)
+        s = "a%d%d" % (slot, 0 if c0 == 0 else 1)
+        lands[r].append((key, slot, c0, c1, s, len(eng)))
+        return (r, buf, "in%d" % slot, c0, c1, eng, s)
+
+    for j in range(n):
+        near = [r for r in users[j] if place(cores[r]) == place(cores[j])]
+        chips = {}
+        for r in users[j]:
+            if r not in near:
+                chips.setdefault(place(cores[r]), []).append(r)
+        groups = list(chips.values())
+        both = [("ldx0", 16), ("ldx1", 16)]
+        if any(len(grp) > 1 for grp in groups):
+            heads = [sorted(grp, key=lambda r: (not users[r], topo.die(cores[r]) != topo.die(cores[j]), r))[0]
+                     for grp in groups]
+            first = [move(j, "xs", j, h, 0, HALF, e, 2) for h, e in zip(heads, _share(offchip[j], len(heads)))]
+            calls[j].append((both[:1], first))
+            for h, grp, tr in zip(heads, groups, first):
+                rest = [r for r in grp if r != h]
+                if rest:
+                    later[h].append(([(tr[6], len(tr[5]))],
+                                     [move(h, tr[2], j, r, 0, HALF, e, 4)
+                                      for r, e in zip(rest, _share(onchip(h, rest), len(rest)))]))
+            allfar = [r for grp in groups for r in grp]
+            calls[j].append((both[1:], [move(j, "xs", j, r, HALF, TK, e, 5)
+                                        for r, e in zip(allfar, _share(offchip[j], len(allfar)))]))
+        elif groups:
+            allfar = [r for grp in groups for r in grp]
+            calls[j].append((both, [move(j, "xs", j, r, 0, TK, e, 3)
+                                    for r, e in zip(allfar, _share(offchip[j], len(allfar)))]))
+        if near:
+            calls[j].append((both, [move(j, "xs", j, r, 0, TK, e, 1)
+                                    for r, e in zip(near, _share(onchip(j, near), len(near)))]))
+    return users, [calls[j] + later[j] for j in range(n)], lands
 
 
 def rank_program(g, core, T, topo):
@@ -61,57 +102,51 @@ def rank_program(g, core, T, topo):
     if r is None:
         return
     mask, cores, sem = T.tables["MASK"], T.cores, T.sem
-    calls = _plan(T, topo, r)
+    users, calls, lands = _plan(T, topo)
+    own = r in mask[r]
 
-    if calls or r in mask[r]:
-        g.sync.dma_start(T.xs[:], T.x[:]).then_inc(sem.ldx, 16)
+    if users[r] or own:
+        for c in range(2):
+            g.sync.dma_start(T.xs[:, c * HALF:(c + 1) * HALF], T.x[:, c * HALF:(c + 1) * HALF]).then_inc(sem["ldx%d" % c], 16)
     g.sync.dma_start(T.ws[:], T.w[:]).then_inc(sem.ldw, 16)
 
-    if calls:
-        g.wait_ge(sem.ldx, 16)
-        total = 0
-        for call in calls:
-            trs = []
-            for d, slot, eng in call:
-                rid, pid = topo.addr(cores[d], core)
-                trs.append(RemoteDMATransfer(dst_ids=[DstId(rid=rid, pnc=pid)],
-                                             dma_engine_mask=sum(1 << e for e in eng),
-                                             remote_sem=sem["arr%d" % slot],
-                                             src=T.xs[:], dst=T["in%d" % slot][:]))
-                total += len(eng)
-            g.remote_dma_fused(trs, local_sem=sem.sent)
+    total = 0
+    for waits, trs in calls[r]:
+        for s, c in waits:
+            g.wait_ge(sem[s], c)
+        lst = []
+        for d, src, dst, c0, c1, eng, s in trs:
+            rid, pid = topo.addr(cores[d], core)
+            lst.append(RemoteDMATransfer(dst_ids=[DstId(rid=rid, pnc=pid)], dma_engine_mask=sum(1 << e for e in eng),
+                                         remote_sem=sem[s], src=T[src][:, c0:c1], dst=T[dst][:, c0:c1]))
+            total += len(eng)
+        g.remote_dma_fused(lst, local_sem=sem.sent)
+    if total:
         g.wait_ge(sem.sent, total)
 
-    terms = []
-    for i, j in enumerate(mask[r]):
-        if j == r:
-            terms.append((0, 0, i, 0))
-            continue
-        for call in _plan(T, topo, j):
-            for d, slot, eng in call:
-                if d == r:
-                    terms.append((1 if _same_chip(topo, cores[j], core) else 2, 128 // len(eng), i, len(eng)))
+    terms = [(k, slot, c0, c1, s, c, "in%d" % slot) for k, slot, c0, c1, s, c in lands[r]]
+    if own:
+        terms += [(0, mask[r].index(r), c * HALF, (c + 1) * HALF, "ldx%d" % c, 16, "xs") for c in range(2)]
     terms.sort()
-
-    te = g.tensor
+    te, cnt, done = g.tensor, [0] * NP, []
     te.wait_ge(sem.ldw, 16)
-    for k, (_, _, i, cnt) in enumerate(terms):
-        if cnt == 0:
-            te.wait_ge(sem.ldx, 16)
-            rhs = T.xs
-        else:
-            te.wait_ge(sem["arr%d" % i], cnt)
-            rhs = T["in%d" % i]
-        last = k == len(terms) - 1
-        for p in range(PIECES):
-            ins = te.matmul(T["ps%d" % p][:, 0:CW], T.ws[:, TILE * i:TILE * (i + 1)], rhs[:, p * CW:(p + 1) * CW],
-                            k == 0, last)
-            if last:
+    for _, slot, c0, c1, s, c, buf in terms:
+        te.wait_ge(sem[s], c)
+        for p in range(c0 // PW, c1 // PW):
+            ins = te.matmul(T["ps%d" % p][:, 0:PW], T.ws[:, TILE * slot:TILE * (slot + 1)],
+                            T[buf][:, p * PW:(p + 1) * PW], cnt[p] == 0, cnt[p] == DEG - 1)
+            cnt[p] += 1
+            if cnt[p] == DEG:
                 ins.then_inc(sem["mm%d" % p], 1)
+                done.append(p)
 
-    for p in range(PIECES):
+    left = [HALF // PW, HALF // PW]
+    for p in done:
+        h = p * PW // HALF
         g.vector.wait_ge(sem["mm%d" % p], 1)
-        g.vector.tensor_copy(T.ys[:, p * CW:(p + 1) * CW], T["ps%d" % p][:, 0:CW]).then_inc(sem.cp, 1)
-    g.sync.wait_ge(sem.cp, PIECES)
-    g.sync.dma_start(T.y[:], T.ys[:]).then_inc(sem.st, 16)
-    g.sync.wait_ge(sem.st, 16)
+        g.vector.tensor_copy(T.ys[:, p * PW:(p + 1) * PW], T["ps%d" % p][:, 0:PW]).then_inc(sem["cp%d" % h], 1)
+        left[h] -= 1
+        if left[h] == 0:
+            g.sync.wait_ge(sem["cp%d" % h], HALF // PW)
+            g.sync.dma_start(T.y[:, h * HALF:(h + 1) * HALF], T.ys[:, h * HALF:(h + 1) * HALF]).then_inc(sem.st, 16)
+    g.sync.wait_ge(sem.st, 32)

from concourse.bass import DstId, RemoteDMATransfer

DEG, TILE, TK = 3, 128, 512
HALF = TK // 2
PW = 128
NP = TK // PW

SCRATCH = {
    "xs": ("sbuf", [128, TK], "bfloat16"),
    "ws": ("sbuf", [128, DEG * TILE], "bfloat16"),
    "ys": ("sbuf", [128, TK], "bfloat16"),
}
for _i in range(DEG):
    SCRATCH["in%d" % _i] = ("sbuf", [128, TK], "bfloat16")
for _p in range(NP):
    SCRATCH["ps%d" % _p] = ("psum", [128, 512], "float32")

SEMAPHORES = (["ldx0", "ldx1", "ldw", "sent", "cp0", "cp1", "st"]
              + ["a%d%d" % (_i, _c) for _i in range(DEG) for _c in range(2)]
              + ["mm%d" % _p for _p in range(NP)])


def _bits(m):
    return [b for b in range(m.bit_length()) if (m >> b) & 1]


def _pow2(n):
    p = 1
    while 2 * p <= n:
        p *= 2
    return p


def _share(engines, k):
    n = _pow2(len(engines) // k)
    return [engines[i * n:(i + 1) * n] for i in range(k)]


def _plan(T, topo):
    mask, cores = T.tables["MASK"], T.cores
    n = len(cores)

    def place(c):
        return (topo.host(c), topo.chip(c))

    users = [[r for r in range(n) if r != j and j in mask[r]] for j in range(n)]
    calls, later, lands, offchip = [[] for _ in range(n)], [[] for _ in range(n)], [[] for _ in range(n)], []
    for j in range(n):
        eng = None
        for r in users[j]:
            if place(cores[r]) != place(cores[j]):
                b = _bits(topo.mask(cores[j], cores[r]))
                eng = b if eng is None else [e for e in eng if e in b]
        offchip.append(eng or [])

    def onchip(q, dsts):
        eng = _bits(topo.mask(cores[q], cores[dsts[0]]))
        for d in dsts[1:]:
            eng = [e for e in eng if e in _bits(topo.mask(cores[q], cores[d]))]
        return [e for e in eng if e not in offchip[q]] or eng

    def move(q, buf, j, r, c0, c1, eng, key):
        slot = mask[r].index(j)
        s = "a%d%d" % (slot, 0 if c0 == 0 else 1)
        lands[r].append((key, slot, c0, c1, s, len(eng)))
        return (r, buf, "in%d" % slot, c0, c1, eng, s)

    for j in range(n):
        near = [r for r in users[j] if place(cores[r]) == place(cores[j])]
        chips = {}
        for r in users[j]:
            if r not in near:
                chips.setdefault(place(cores[r]), []).append(r)
        groups = list(chips.values())
        both = [("ldx0", 16), ("ldx1", 16)]
        if any(len(grp) > 1 for grp in groups):
            heads = [sorted(grp, key=lambda r: (not users[r], topo.die(cores[r]) != topo.die(cores[j]), r))[0]
                     for grp in groups]
            first = [move(j, "xs", j, h, 0, HALF, e, 2) for h, e in zip(heads, _share(offchip[j], len(heads)))]
            calls[j].append((both[:1], first))
            for h, grp, tr in zip(heads, groups, first):
                rest = [r for r in grp if r != h]
                if rest:
                    later[h].append(([(tr[6], len(tr[5]))],
                                     [move(h, tr[2], j, r, 0, HALF, e, 4)
                                      for r, e in zip(rest, _share(onchip(h, rest), len(rest)))]))
            allfar = [r for grp in groups for r in grp]
            calls[j].append((both[1:], [move(j, "xs", j, r, HALF, TK, e, 5)
                                        for r, e in zip(allfar, _share(offchip[j], len(allfar)))]))
        elif groups:
            allfar = [r for grp in groups for r in grp]
            calls[j].append((both, [move(j, "xs", j, r, 0, TK, e, 3)
                                    for r, e in zip(allfar, _share(offchip[j], len(allfar)))]))
        if near:
            calls[j].append((both, [move(j, "xs", j, r, 0, TK, e, 1)
                                    for r, e in zip(near, _share(onchip(j, near), len(near)))]))
    return users, [calls[j] + later[j] for j in range(n)], lands


def rank_program(g, core, T, topo):
    r = T.rank_of(core)
    if r is None:
        return
    mask, cores, sem = T.tables["MASK"], T.cores, T.sem
    users, calls, lands = _plan(T, topo)
    own = r in mask[r]

    if users[r] or own:
        for c in range(2):
            g.sync.dma_start(T.xs[:, c * HALF:(c + 1) * HALF], T.x[:, c * HALF:(c + 1) * HALF]).then_inc(sem["ldx%d" % c], 16)
    g.sync.dma_start(T.ws[:], T.w[:]).then_inc(sem.ldw, 16)

    total = 0
    for waits, trs in calls[r]:
        for s, c in waits:
            g.wait_ge(sem[s], c)
        lst = []
        for d, src, dst, c0, c1, eng, s in trs:
            rid, pid = topo.addr(cores[d], core)
            lst.append(RemoteDMATransfer(dst_ids=[DstId(rid=rid, pnc=pid)], dma_engine_mask=sum(1 << e for e in eng),
                                         remote_sem=sem[s], src=T[src][:, c0:c1], dst=T[dst][:, c0:c1]))
            total += len(eng)
        g.remote_dma_fused(lst, local_sem=sem.sent)
    if total:
        g.wait_ge(sem.sent, total)

    terms = [(k, slot, c0, c1, s, c, "in%d" % slot) for k, slot, c0, c1, s, c in lands[r]]
    if own:
        terms += [(0, mask[r].index(r), c * HALF, (c + 1) * HALF, "ldx%d" % c, 16, "xs") for c in range(2)]
    terms.sort()
    te, cnt, done = g.tensor, [0] * NP, []
    te.wait_ge(sem.ldw, 16)
    for _, slot, c0, c1, s, c, buf in terms:
        te.wait_ge(sem[s], c)
        for p in range(c0 // PW, c1 // PW):
            ins = te.matmul(T["ps%d" % p][:, 0:PW], T.ws[:, TILE * slot:TILE * (slot + 1)],
                            T[buf][:, p * PW:(p + 1) * PW], cnt[p] == 0, cnt[p] == DEG - 1)
            cnt[p] += 1
            if cnt[p] == DEG:
                ins.then_inc(sem["mm%d" % p], 1)
                done.append(p)

    left = [HALF // PW, HALF // PW]
    for p in done:
        h = p * PW // HALF
        g.vector.wait_ge(sem["mm%d" % p], 1)
        g.vector.tensor_copy(T.ys[:, p * PW:(p + 1) * PW], T["ps%d" % p][:, 0:PW]).then_inc(sem["cp%d" % h], 1)
        left[h] -= 1
        if left[h] == 0:
            g.sync.wait_ge(sem["cp%d" % h], HALF // PW)
            g.sync.dma_start(T.y[:, h * HALF:(h + 1) * HALF], T.ys[:, h * HALF:(h + 1) * HALF]).then_inc(sem.st, 16)
    g.sync.wait_ge(sem.st, 32)
